import numpy as np
import ml_dtypes


def mxq(x, axis, fmt="e4m3"):
    dtype, down = {"e4m3": (ml_dtypes.float8_e4m3fn, 7), "e5m2": (ml_dtypes.float8_e5m2, 14)}[fmt]
    v = np.moveaxis(np.asarray(x, np.float32).astype(ml_dtypes.bfloat16).astype(np.float64), axis, -1)
    blocks = v.reshape(v.shape[:-1] + (-1, 32))
    amax = np.abs(blocks).max(-1, keepdims=True)
    byte = np.maximum(np.where(amax > 0, np.frexp(amax)[1] - 1 + 127, 0) - down, 1)
    scale = np.exp2(byte - 127.0)
    codes = (blocks / scale).astype(np.float32).astype(dtype).astype(np.float64)
    return np.moveaxis((codes * scale).reshape(v.shape), -1, axis)


WIDE = False


def mx_kscale(k):
    if not WIDE:
        return np.ones(k)
    levels = np.array([10, -10, 5, -5, 0])
    if k % 512:
        return np.exp2(np.random.permutation(np.resize(levels, k // 32))).repeat(32)
    a = np.empty((k // 512, 16))
    for p in range(k // 512):
        a[p, :8] = np.random.permutation(np.resize(levels, 8))
        for g in range(8):
            far = levels[np.abs(levels - a[p, g]) >= 10]
            a[p, g + 8] = far[np.random.randint(len(far))]
    return np.exp2(a.ravel()).repeat(32)


BF16 = ml_dtypes.bfloat16


def bf(x):
    return np.asarray(x, np.float32).astype(BF16)


def f64(x):
    return np.asarray(x).astype(np.float64)

def planes(Y):
    n, m = Y.shape
    b = f64(bf(Y)).reshape(n // 32, 32, m)
    amax = np.abs(b).max(1)
    byte = np.clip(np.where(amax > 0, np.frexp(amax)[1] - 1 + 127 - 7, 1), 1, 254)
    codes = (b * np.exp2(127.0 - byte)[:, None, :]).reshape(n, m).astype(np.float32).astype(ml_dtypes.float8_e4m3fn).view(np.uint8)
    words = codes.reshape(n // 512, 128, 4, m).transpose(0, 1, 3, 2)
    return np.ascontiguousarray(words), np.ascontiguousarray(byte.astype(np.uint8).reshape(n // 512, 16, m))


P, U, G, I, D = 2, 1024, 512, 1024, 256

NEG_SLOPE = 0.2


def leaky(t):
    return np.where(t >= 0, t, NEG_SLOPE * t)


def setup_inputs():
    s, t = mx_kscale(U), mx_kscale(G)
    hu = np.random.standard_normal((P, U, G)) / np.sqrt(U)
    eu = np.random.standard_normal((P, U, D))
    wg = 1.0 + 0.1 * np.random.standard_normal((P, G))
    hi = np.random.standard_normal((P, I, G)) / np.sqrt(G)
    ei = np.random.standard_normal((P, I, D))
    return {"hu": bf(hu * s[:, None]), "eu": bf(eu / s[:, None]), "wg": bf(wg * t), "hi": bf(hi / t), "ei": bf(ei)}


def core(hu, eu, wg, hi, ei):
    r = mxq(f64(hu), 1, "e4m3").transpose(0, 2, 1) @ mxq(f64(eu), 1, "e4m3")
    z = leaky(r)
    zw = f64(wg)[:, :, None] * z
    m = mxq(f64(hi), 2, "e4m3") @ mxq(zw, 1, "e4m3")
    return leaky(m) + m * f64(ei)


def reference(hu, eu, wg, hi, ei):
    R_out = core(hu, eu, wg, hi, ei)
    words, scales = planes(np.moveaxis(R_out, 1, 0).reshape(1024, -1))
    return R_out, words, scales

from contextlib import ExitStack

import concourse.mybir as mybir
from concourse.masks import make_identity

P, U, G, I, D = 2, 1024, 512, 1024, 256
FLOPS = 2 * P * U * G * D + 2 * P * I * G * D

F32 = mybir.dt.float32
BF16 = mybir.dt.bfloat16
U32 = mybir.dt.uint32
I32 = mybir.dt.int32
U8 = mybir.dt.uint8
FP8X4 = mybir.dt.float8_e4m3fn_x4
ALU = mybir.AluOpType
ACT = mybir.ActivationFunctionType

HALF = 128
GROUP = 512
HALVES = range(2)

SCALAR_SHARE = {(0, 0): 48, (0, 1): 24, (1, 0): 56, (1, 1): 80}


def four_rows(x, p, g):
    return x[p, GROUP * g : GROUP * (g + 1), :].rearrange("(m t) w -> m t w", t=4)


def tile_usergrouphyperedgetoitempropagation_x1_kernel(tc, hu, eu, wg, hi, ei, out_0, out_1, out_2):
    nc = tc.nc
    with ExitStack() as ctx:
        keep = ctx.enter_context(tc.tile_pool(name="keep", bufs=1))
        psum_r = ctx.enter_context(tc.psum_pool(name="psum_r", bufs=2))
        psum_turn = ctx.enter_context(tc.psum_pool(name="psum_turn", bufs=3))
        psum_m = ctx.enter_context(tc.psum_pool(name="psum_m", bufs=3))

        def tiles(name, keys, shape, dt):
            return {k: keep.tile(shape, dt, name="%s_%d" % (name, i), align_bytes=64) for i, k in enumerate(keys)}

        graphs = range(P)
        groups = range(2)
        pairs = [(p, g) for p in graphs for g in groups]
        thirds = [(p, g, h) for p, g in pairs for h in HALVES]
        stage1 = [(p, h) for p in graphs for h in HALVES]

        eu_rows = tiles("eu_rows", pairs, [128, 4, D], BF16)
        hu_rows = tiles("hu_rows", pairs, [128, 4, G], BF16)
        hi_rows = tiles("hi_rows", pairs, [128, 4, G], BF16)
        ei_rows = tiles("ei_rows", pairs, [128, 4, D], BF16)
        wg_slots = keep.tile([128, P, 4], BF16, name="wg_slots", align_bytes=64)
        ident = keep.tile([128, 128], F32, name="ident", align_bytes=64)

        eu_four = tiles("eu_four", pairs, [128, D, 4], BF16)
        hu_four = tiles("hu_four", pairs, [128, 4, 128, 4], BF16)
        hi_four = tiles("hi_four", pairs, [128, 4, 128, 4], BF16)
        zw_four = tiles("zw_four", graphs, [128, D, 4], BF16)
        out_four = tiles("out_four", pairs, [128, D, 4], BF16)
        eu_codes = tiles("eu_codes", pairs, [128, D], U32)
        hu_codes = tiles("hu_codes", pairs, [128, G], U32)
        hi_codes = tiles("hi_codes", pairs, [128, GROUP], U32)
        zw_codes = tiles("zw_codes", graphs, [128, D], U32)
        out_codes = tiles("out_codes", groups, [128, P * D], U32)
        eu_scales = tiles("eu_scales", pairs, [128, D], U8)
        hu_scales = tiles("hu_scales", pairs, [128, G], U8)
        hi_scales = tiles("hi_scales", pairs, [128, GROUP], U8)
        zw_scales = tiles("zw_scales", graphs, [128, D], U8)
        out_scales = tiles("out_scales", groups, [128, P * D], U8)

        relu_r = tiles("relu_r", stage1, [128, HALF, 4], F32)
        leaky_r = tiles("leaky_r", stage1, [128, HALF, 4], F32)
        ei_term = tiles("ei_term", thirds, [128, 4, HALF], F32)
        factor = tiles("factor", thirds, [128, 4, HALF], F32)
        out_rows = tiles("out_rows", pairs, [128, 4, D], F32)

        r_banks, m_banks = {}, {}

        def cols(h):
            return slice(HALF * h, HALF * (h + 1))

        def copy(engine, out, in_):
            if engine == "scalar":
                nc.scalar.copy(out=out, in_=in_)
            else:
                nc.vector.tensor_copy(out=out, in_=in_)

        def quantise(codes, scales, four):
            nc.vector.quantize_mx(out=codes.bitcast(FP8X4), scales=scales, in_=four)

        def interleave_eu(p, g, engine):
            copy(
                engine,
                eu_four[p, g][:].rearrange("q (c i) j -> q c j i", i=4),
                eu_rows[p, g][:].rearrange("q j (c i) -> q c j i", i=4),
            )

        def interleave_hu(p, g):
            rows = hu_rows[p, g][:].rearrange("q j (m t) -> q m j t", t=4)
            four = hu_four[p, g][:].rearrange("q t m j -> q m j t")
            cut = SCALAR_SHARE[p, g]
            copy("scalar", four[:, :cut], rows[:, :cut])
            copy("vector", four[:, cut:], rows[:, cut:])

        def quantise_eu(p, g):
            quantise(eu_codes[p, g][:], eu_scales[p, g][:], eu_four[p, g][:].rearrange("q d j -> q (d j)"))

        def quantise_hu(p, g):
            quantise(hu_codes[p, g][:], hu_scales[p, g][:], hu_four[p, g][:].rearrange("q t m j -> q (t m j)"))

        def turn_hi(p, g):
            banks = []
            for b in range(2):
                bank = psum_turn.tile([128, 2, 2, 128], F32, name="turned")
                for s in range(2):
                    words = hi_rows[p, g][:, 2 * b + s, :].bitcast(F32)
                    for u in range(2):
                        nc.tensor.transpose(bank[:, s, u, :], words[:, u : G // 2 : 2], ident[:])
                banks.append(bank)
            return banks

        def empty_turned(p, g, banks):
            words = hi_four[p, g][:].rearrange("q t m j -> q (t m j)").bitcast(F32).rearrange("q (t m u) -> q t m u", t=4, u=2)
            for b in range(2):
                nc.scalar.copy(out=words[:, 2 * b : 2 * b + 2], in_=banks[b][:].rearrange("q t u m -> q t m u"))

        def quantise_hi(p, g):
            quantise(hi_codes[p, g][:], hi_scales[p, g][:], hi_four[p, g][:].rearrange("q t m j -> q (t m j)"))

        def multiply_r(p):
            for h in HALVES:
                bank = psum_r.tile([128, 4, HALF], F32, name="r")
                r_banks[p, h] = bank
                for t in range(4):
                    for g in groups:
                        nc.tensor.matmul_mx(
                            out=bank[:, t, :],
                            lhsT=hu_codes[p, g][:, 128 * t : 128 * (t + 1)].bitcast(FP8X4),
                            lhsT_scale=hu_scales[p, g][:, 128 * t : 128 * (t + 1)],
                            rhs=eu_codes[p, g][:, cols(h)].bitcast(FP8X4),
                            rhs_scale=eu_scales[p, g][:, cols(h)],
                            start=(g == 0),
                            stop=(g == 1),
                        )

        def relu_of_r(p):
            for h in HALVES:
                nc.scalar.activation(
                    out=relu_r[p, h][:], in_=r_banks[p, h][:].rearrange("m t d -> m d t"), func=ACT.Relu, scale=0.8
                )

        def leaky_of_r(p):
            for h in HALVES:
                nc.vector.scalar_tensor_tensor(
                    out=leaky_r[p, h][:],
                    in0=r_banks[p, h][:].rearrange("m t d -> m d t"),
                    scalar=0.2,
                    in1=relu_r[p, h][:],
                    op0=ALU.mult,
                    op1=ALU.add,
                )

        def weight_z(p):
            for h in HALVES:
                nc.vector.tensor_tensor(
                    out=zw_four[p][:, cols(h), :],
                    in0=leaky_r[p, h][:],
                    in1=wg_slots[:, p, :].unsqueeze(1).to_broadcast([128, HALF, 4]),
                    op=ALU.mult,
                )

        def quantise_zw(p):
            for h in HALVES:
                four = zw_four[p][:, cols(h), :].rearrange("q d t -> q (d t)")
                quantise(zw_codes[p][:, cols(h)], zw_scales[p][:, cols(h)], four)

        def multiply_m(p, g):
            for h in HALVES:
                bank = psum_m.tile([128, 4, HALF], F32, name="m")
                m_banks[p, g, h] = bank
                for t in range(4):
                    nc.tensor.matmul_mx(
                        out=bank[:, t, :],
                        lhsT=hi_codes[p, g][:, 128 * t : 128 * (t + 1)].bitcast(FP8X4),
                        lhsT_scale=hi_scales[p, g][:, 128 * t : 128 * (t + 1)],
                        rhs=zw_codes[p][:, cols(h)].bitcast(FP8X4),
                        rhs_scale=zw_scales[p][:, cols(h)],
                        start=True,
                        stop=True,
                    )

        def term_of_ei(p, g):
            for h in HALVES:
                nc.scalar.activation(out=ei_term[p, g, h][:], in_=ei_rows[p, g][:, :, cols(h)], func=ACT.Copy, scale=1.25, bias=0.25)

        def factor_of_m(p, g):
            for h in HALVES:
                nc.vector.scalar_tensor_tensor(
                    out=factor[p, g, h][:], in0=m_banks[p, g, h][:], scalar=0.0, in1=ei_term[p, g, h][:], op0=ALU.is_ge, op1=ALU.add
                )

        def finish_out(p, g):
            for h in HALVES:
                nc.vector.scalar_tensor_tensor(
                    out=out_rows[p, g][:, :, cols(h)],
                    in0=factor[p, g, h][:],
                    scalar=0.8,
                    in1=m_banks[p, g, h][:],
                    op0=ALU.mult,
                    op1=ALU.mult,
                )
            nc.sync.dma_start(out=four_rows(out_0, p, g), in_=out_rows[p, g][:])

        def interleave_out(p, g, engine):
            for h in HALVES:
                copy(
                    engine,
                    out_four[p, g][:, cols(h), :].rearrange("q (c i) t -> q c t i", i=4),
                    out_rows[p, g][:, :, cols(h)].rearrange("q t (c i) -> q c t i", i=4),
                )

        def quantise_out(p, g):
            for h in HALVES:
                span = slice(D * p + HALF * h, D * p + HALF * (h + 1))
                quantise(out_codes[g][:, span], out_scales[g][:, span], out_four[p, g][:, cols(h), :].rearrange("q d t -> q (d t)"))
            words = out_1[g].rearrange("q m t -> q (m t)").bitcast(I32)
            nc.sync.dma_start(out=words[:, D * p : D * (p + 1)], in_=out_codes[g][:, D * p : D * (p + 1)].bitcast(I32))

        def store_scales(g):
            for q in range(4):
                nc.scalar.dma_start(
                    out=out_2[g, 4 * q : 4 * q + 4, :].bitcast(I32), in_=out_scales[g][32 * q : 32 * q + 4, :].bitcast(I32)
                )

        make_identity(nc, ident[:])

        with tc.manual_schedule():
            def load(rows, x, p, g):
                nc.sync.dma_start(out=rows[p, g][:], in_=four_rows(x, p, g))

            load(hu_rows, hu, 0, 0)
            load(hu_rows, hu, 0, 1)
            load(hi_rows, hi, 0, 0)
            load(eu_rows, eu, 0, 0)
            load(eu_rows, eu, 0, 1)
            load(hu_rows, hu, 1, 0)
            load(eu_rows, eu, 1, 1)
            nc.sync.dma_start(out=wg_slots[:], in_=wg.rearrange("p (m t) -> m p t", t=4))
            load(hu_rows, hu, 1, 1)
            load(hi_rows, hi, 0, 1)
            load(eu_rows, eu, 1, 0)
            load(hi_rows, hi, 1, 0)
            load(ei_rows, ei, 0, 0)
            load(ei_rows, ei, 1, 0)
            load(ei_rows, ei, 0, 1)
            load(ei_rows, ei, 1, 1)
            load(hi_rows, hi, 1, 1)

            interleave_hu(0, 0)
            interleave_hu(0, 1)
            quantise_hu(0, 0)
            quantise_hu(0, 1)
            turned = turn_hi(0, 0)
            interleave_eu(0, 0, "scalar")
            interleave_eu(0, 1, "vector")
            quantise_eu(0, 0)
            quantise_eu(0, 1)
            empty_turned(0, 0, turned)
            multiply_r(0)
            turned = turn_hi(0, 1)

            interleave_hu(1, 0)
            quantise_hi(0, 0)
            interleave_eu(1, 1, "vector")
            quantise_hu(1, 0)
            relu_of_r(0)
            leaky_of_r(0)
            weight_z(0)
            quantise_zw(0)
            interleave_hu(1, 1)
            quantise_eu(1, 1)
            quantise_hu(1, 1)
            interleave_eu(1, 0, "scalar")
            quantise_eu(1, 0)

            multiply_m(0, 0)
            term_of_ei(0, 0)
            factor_of_m(0, 0)
            empty_turned(0, 1, turned)
            quantise_hi(0, 1)
            finish_out(0, 0)
            turned = turn_hi(1, 0)
            multiply_m(0, 1)
            term_of_ei(0, 1)
            factor_of_m(0, 1)
            finish_out(0, 1)
            term_of_ei(1, 0)
            empty_turned(1, 0, turned)
            quantise_hi(1, 0)

            multiply_r(1)
            relu_of_r(1)
            turned = turn_hi(1, 1)
            leaky_of_r(1)
            weight_z(1)
            quantise_zw(1)
            interleave_out(0, 0, "scalar")
            quantise_out(0, 0)
            empty_turned(1, 1, turned)
            quantise_hi(1, 1)

            multiply_m(1, 0)
            interleave_out(0, 1, "scalar")
            term_of_ei(1, 1)
            factor_of_m(1, 0)
            finish_out(1, 0)
            multiply_m(1, 1)
            factor_of_m(1, 1)
            interleave_out(1, 0, "scalar")
            quantise_out(0, 1)
            quantise_out(1, 0)
            finish_out(1, 1)
            store_scales(0)
            interleave_out(1, 1, "vector")
            quantise_out(1, 1)
            store_scales(1)
